import numpy as np
import ml_dtypes


def mxq(x, axis, fmt="e4m3"):
    dtype, down = {"e4m3": (ml_dtypes.float8_e4m3fn, 7), "e5m2": (ml_dtypes.float8_e5m2, 14)}[fmt]
    v = np.moveaxis(np.asarray(x, np.float32).astype(ml_dtypes.bfloat16).astype(np.float64), axis, -1)
    blocks = v.reshape(v.shape[:-1] + (-1, 32))
    amax = np.abs(blocks).max(-1, keepdims=True)
    byte = np.maximum(np.where(amax > 0, np.frexp(amax)[1] - 1 + 127, 0) - down, 1)
    scale = np.exp2(byte - 127.0)
    codes = (blocks / scale).astype(np.float32).astype(dtype).astype(np.float64)
    return np.moveaxis((codes * scale).reshape(v.shape), -1, axis)


WIDE = False


def mx_kscale(k):
    if not WIDE:
        return np.ones(k)
    levels = np.array([10, -10, 5, -5, 0])
    if k % 512:
        return np.exp2(np.random.permutation(np.resize(levels, k // 32))).repeat(32)
    a = np.empty((k // 512, 16))
    for p in range(k // 512):
        a[p, :8] = np.random.permutation(np.resize(levels, 8))
        for g in range(8):
            far = levels[np.abs(levels - a[p, g]) >= 10]
            a[p, g + 8] = far[np.random.randint(len(far))]
    return np.exp2(a.ravel()).repeat(32)


def f64(x):
    return np.asarray(x).astype(np.float64)


def striped(idx):
    return np.tile(idx.reshape(-1, 16).T, (8, 1)).astype(np.uint16)


def unstriped(offs):
    return offs[:16].T.reshape(-1).astype(np.int64)


def pack_weight(w):
    k, n = w.shape
    w = f64(np.asarray(w, np.float32).astype(ml_dtypes.bfloat16)).reshape(k // 32, 32, n)
    amax = np.abs(w).max(1)
    byte = np.clip(np.where(amax > 0, np.frexp(amax)[1] - 1 + 127 - 7, 1), 1, 254)
    scaled = (w * np.exp2(127.0 - byte)[:, None, :]).reshape(k, n).astype(np.float32)
    words = np.ascontiguousarray(scaled.reshape(k // 512, 128, 4, n).transpose(0, 1, 3, 2)).astype(ml_dtypes.float8_e4m3fn).view(np.uint8)
    return words, np.ascontiguousarray(byte.astype(np.uint8).reshape(k // 512, 16, n))


def unpack_weight(words, scales):
    g, p, n, _ = words.shape
    vals = np.ascontiguousarray(words).view(ml_dtypes.float8_e4m3fn).astype(np.float64) * np.repeat(np.exp2(scales.astype(np.float64) - 127.0), 8, axis=1)[..., None]
    return vals.transpose(0, 1, 3, 2).reshape(g * 512, n)


E2M1 = np.array([0.0, 0.5, 1.0, 1.5, 2.0, 3.0, 4.0, 6.0, -0.0, -0.5, -1.0, -1.5, -2.0, -3.0, -4.0, -6.0])


def pack_fp4(w):
    k, n = w.shape
    w = f64(np.asarray(w, np.float32).astype(ml_dtypes.bfloat16)).reshape(k // 32, 32, n)
    amax = np.abs(w).max(1)
    mant, ex = np.frexp(amax / 6.0)
    byte = np.clip(np.where(amax > 0, np.where(mant > 0.5, ex, ex - 1) + 127, 1), 1, 254)
    scaled = (w * np.exp2(127.0 - byte)[:, None, :]).reshape(k, n).astype(np.float32)
    c = np.ascontiguousarray(scaled.reshape(k // 512, 128, 4, n).transpose(0, 1, 3, 2)).astype(ml_dtypes.float4_e2m1fn).view(np.uint8) & 0xF
    words = (c[..., 0::2] | (c[..., 1::2] << 4)).reshape(k // 512, 128, 2 * n)
    return np.ascontiguousarray(words), np.ascontiguousarray(byte.astype(np.uint8).reshape(k // 512, 16, n))


def unpack_fp4(words, scales):
    g, _, n = scales.shape
    words = np.ascontiguousarray(words).reshape(g, 128, n, 2)
    nib = np.empty((g, 128, n, 4), np.uint8)
    nib[..., 0::2] = words & 0xF
    nib[..., 1::2] = words >> 4
    vals = E2M1[nib] * np.repeat(np.exp2(scales.astype(np.float64) - 127.0), 8, axis=1)[..., None]
    return vals.transpose(0, 1, 3, 2).reshape(g * 512, n)


K, T, S, N, H = 512, 1024, 512, 256, 512


def setup_inputs():
    n = np.random.standard_normal
    s = mx_kscale(K)[:, None]
    u = mx_kscale(H)
    packed_xT = pack_weight(n((K, T)) * s)
    packed_w1 = pack_fp4(n((K, H)) / np.sqrt(K) / s)
    packed_w2 = pack_fp4(n((K, H)) / np.sqrt(K) / s)
    packed_w3 = pack_fp4(n((H, N)) / np.sqrt(H) / u[:, None])
    return {
        "x_words": packed_xT[0],
        "x_scales": packed_xT[1],
        "w1_words": packed_w1[0],
        "w1_scales": packed_w1[1],
        "w2_words": packed_w2[0],
        "w2_scales": packed_w2[1],
        "unit": (np.random.uniform(0.6, 1.4, (H, 1)) * u[:, None]).astype(np.float32),
        "w3_words": packed_w3[0],
        "w3_scales": packed_w3[1],
        "offs": striped(np.random.permutation(T)[:S]),
        "nxt": striped(np.random.permutation(S)),
        "prv": striped(np.random.permutation(S)),
    }


def reference(x_words, x_scales, w1_words, w1_scales, w2_words, w2_scales, unit, w3_words, w3_scales, offs, nxt, prv):
    xq = unpack_weight(x_words, x_scales)[:, unstriped(offs)]
    px = unpack_fp4(w1_words, w1_scales).T @ xq
    xnxt = px[:, unstriped(nxt)]
    dnxt = xnxt - px
    py = unpack_fp4(w2_words, w2_scales).T @ xq
    ynxt = py[:, unstriped(nxt)]
    enxt = ynxt - py
    r2 = (dnxt) ** 2 + (enxt) ** 2
    fene = dnxt / (-0.9 * (r2 / (r2 + 4.0)) + 1.0)
    vir = fene * dnxt
    xprv = px[:, unstriped(prv)]
    dprv = xprv - px
    yprv = py[:, unstriped(prv)]
    eprv = yprv - py
    dot = dnxt * dprv + enxt * eprv
    bn = dot[:, unstriped(nxt)]
    hid = f64(unit) * (vir - (0.3 * bn))
    return unpack_fp4(w3_words, w3_scales).T @ mxq(hid, 0, "e4m3")

@@ -1,0 +1,284 @@
+from contextlib import ExitStack
+
+import concourse.mybir as mybir
+from concourse.masks import make_identity
+
+K, T, S, N, H = 512, 1024, 512, 256, 512
+FLOPS = 2 * K * H * S * 2 + 2 * H * N * S
+
+F32 = mybir.dt.float32
+BF16 = mybir.dt.bfloat16
+I32 = mybir.dt.int32
+U32 = mybir.dt.uint32
+U16 = mybir.dt.uint16
+U8 = mybir.dt.uint8
+FP8X4 = mybir.dt.float8_e4m3fn_x4
+FP4X4 = mybir.dt.float4_e2m1fn_x4
+ALU = mybir.AluOpType
+ACT = mybir.ActivationFunctionType
+
+P = 128
+PACK = 4
+HALF = S // 2
+OUT_COLS = 128
+Z_SCALE = 1.140625 / 40.0
+EVAC_S = {(0, 0, 0), (0, 1, 0), (0, 0, HALF)}
+U_S = {3}
+VIR_L0 = {3}
+HOLD = (-1, -1)
+XFIRST = False
+GATHER_V = {(0,1),(0,3),(1,1),(2,1),(3,1)}
+DOT_V = {3}
+SQ_G = {0,1}
+BEND_V = {0}
+SPLITM = False
+IL_S = {1, 3}
+ORDER = "b0 d0 s0 b1 d1 v0 s1 h0 b2 d2 v1 s2 h1 b3 s3 v2 d3 v3 h2 h3"
+
+
+def tile_picked_ypolym_vir_p_kernel(
+    tc, x_words, x_scales, w1_words, w1_scales, w2_words, w2_scales, unit, w3_words, w3_scales, offs, nxt, prv, out
+):
+    nc = tc.nc
+    with ExitStack() as ctx:
+        held = ctx.enter_context(tc.tile_pool(name="held", bufs=1))
+        work = ctx.enter_context(tc.tile_pool(name="work", bufs=4))
+        psum = ctx.enter_context(tc.psum_pool(name="psum", bufs=2))
+
+        offs_sb = held.tile([P, S // 16], U16, name="offs_sb")
+        nxt_sb = held.tile([P, S // 16], U16, name="nxt_sb")
+        prv_sb = held.tile([P, S // 16], U16, name="prv_sb")
+        xw = held.tile([P, T], U32, name="xw", align_bytes=64)
+        xs = held.tile([P, T], U8, name="xs", align_bytes=64)
+        ww = held.tile([P, 2, 2 * H], U8, name="ww", align_bytes=64)
+        w3w = held.tile([P, 2 * N], U8, name="w3w", align_bytes=64)
+        ws = held.tile([P, 2 * H + N], U8, name="ws", align_bytes=64)
+        unit_sb = held.tile([P, PACK], F32, name="unit_sb")
+        coords = held.tile([P, (2 * PACK + 1) * S], F32, name="coords", align_bytes=64)
+        dots = held.tile([P, (PACK + 1) * S], F32, name="dots", align_bytes=64)
+        ident = held.tile([P, P], F32, name="ident", align_bytes=64)
+
+        nc.vector.memset(xs[:].bitcast(I32), 0)
+        nc.vector.memset(ws[:].bitcast(I32), 0)
+        nc.vector.memset(coords[:, 2 * PACK * S :], 0.0)
+        nc.vector.memset(dots[:, PACK * S :], 0.0)
+        make_identity(nc, ident[:])
+
+        def load_scales(queue, dst, src):
+            for q in range(4):
+                queue.dma_start(dst[32 * q : 32 * q + 4, :].bitcast(I32), src[0, 4 * q : 4 * q + 4, :].bitcast(I32))
+
+        nc.sync.dma_start(offs_sb[:], offs)
+        if XFIRST:
+            nc.sync.dma_start(xw[:].bitcast(I32), x_words[0].rearrange("p n t -> p (n t)").bitcast(I32))
+        nc.sync.dma_start(ww[:, 0, :].bitcast(I32), w1_words[0].bitcast(I32))
+        nc.sync.dma_start(ww[:, 1, :].bitcast(I32), w2_words[0].bitcast(I32))
+        if not XFIRST:
+            nc.sync.dma_start(xw[:].bitcast(I32), x_words[0].rearrange("p n t -> p (n t)").bitcast(I32))
+        load_scales(nc.sync, xs, x_scales)
+        load_scales(nc.sync, ws[:, 0:H], w1_scales)
+        load_scales(nc.sync, ws[:, H : 2 * H], w2_scales)
+        nc.sync.dma_start(nxt_sb[:], nxt)
+        nc.sync.dma_start(prv_sb[:], prv)
+        nc.sync.dma_start(unit_sb[:], unit.rearrange("(p t) o -> p (t o)", t=PACK))
+        nc.sync.dma_start(w3w[:].bitcast(I32), w3_words[0].bitcast(I32))
+        load_scales(nc.sync, ws[:, 2 * H :], w3_scales)
+
+        wd = held.tile([P, 2, PACK, 2 * P], U8, name="wd", align_bytes=64)
+        sd = held.tile([P, 2, PACK, P], U8, name="sd", align_bytes=64)
+        for w in range(2):
+            nc.vector.tensor_copy(
+                wd[:, w, :, :].rearrange("p t (m b) -> p t m b", b=2),
+                ww[:, w, :].rearrange("p (m t b) -> p t m b", t=PACK, b=2),
+            )
+
+        xg = held.tile([P, S], U32, name="xg", align_bytes=64)
+        sg = held.tile([P, S], U8, name="sg", align_bytes=64)
+        for h in range(2):
+            cols = slice(h * HALF, (h + 1) * HALF)
+            part = offs_sb[:, h * HALF // 16 : (h + 1) * HALF // 16]
+            nc.vector.tensor_copy(xg[:, cols], xw[:].indirect(part))
+            nc.vector.tensor_copy(sg[:, cols], xs[:].indirect(part))
+            if h == 0:
+                for w in range(2):
+                    nc.vector.tensor_copy(
+                        sd[:, w, :, :], ws[:, w * H : (w + 1) * H].rearrange("p (m t) -> p t m", t=PACK)
+                    )
+
+        vir_unit = held.tile([P, PACK], F32, name="vir_unit")
+        bend_unit = held.tile([P, PACK], F32, name="bend_unit")
+        nc.gpsimd.tensor_scalar(vir_unit[:], unit_sb[:], -360.0 * Z_SCALE, 0.0, ALU.mult, ALU.add)
+        nc.gpsimd.tensor_scalar(bend_unit[:], unit_sb[:], -0.3, 0.0, ALU.mult, ALU.add)
+
+        hid = held.tile([P, PACK, S], F32, name="hid", align_bytes=64)
+
+        def gather(on_vector, dst, window, offsets):
+            if on_vector:
+                nc.vector.tensor_copy(dst, window.indirect(offsets))
+            else:
+                nc.scalar.activation(dst, window.indirect(offsets), ACT.Copy)
+
+        def turn(dst, srcs):
+            for c in range(S // P):
+                cols = slice(c * P, (c + 1) * P)
+                for n, src in enumerate(srcs):
+                    nc.tensor.matmul(
+                        dst[:, cols], lhsT=src[:, cols], rhs=ident[:], start=(n == 0), stop=(n == len(srcs) - 1),
+                        is_transpose=True,
+                    )
+
+        bonds, squares, scaleds, virs, bends = {}, {}, {}, {}, {}
+
+        def make_bonds(t):
+            first = t == 0
+            base = [(2 * (PACK - 1 - t) + 1 - w) * S for w in range(2)]
+            pos = [psum.tile([P, S], F32, name="acc", tag="pos%d" % w) for w in range(2)]
+            widths = [HALF, HALF] if first else [S]
+            c0 = 0
+            for width in widths:
+                cols = slice(c0, c0 + width)
+                for w in range(2):
+                    nc.tensor.matmul_mx(
+                        out=pos[w][:, cols],
+                        lhsT=wd[:, w, t, :].bitcast(FP4X4),
+                        lhsT_scale=sd[:, w, t, :],
+                        rhs=xg[:, cols].bitcast(FP8X4),
+                        rhs_scale=sg[:, cols],
+                        start=True,
+                        stop=True,
+                    )
+                    dst = coords[:, base[w] + c0 : base[w] + c0 + width]
+                    if (t, w, c0) in EVAC_S:
+                        nc.scalar.copy(dst, pos[w][:, cols])
+                    else:
+                        nc.vector.tensor_copy(dst, pos[w][:, cols])
+                c0 += width
+            got = work.tile([P, 4, S], F32, name="got", align_bytes=64)
+            bond = work.tile([P, 4, S], F32, name="bond", align_bytes=64)
+            for n, offsets in enumerate((nxt_sb, prv_sb)):
+                for w in range(2):
+                    window = coords[:, base[w] : base[w] + 2 * S]
+                    gather((t, 2 * n + w) in GATHER_V, got[:, 2 * n + w, :], window, offsets[:])
+                    nc.vector.tensor_tensor(bond[:, 2 * n + w, :], got[:, 2 * n + w, :], pos[w][:], ALU.subtract)
+            bonds[t] = bond
+
+        def make_dot(t):
+            bond = bonds[t]
+            if t == HOLD[1]:
+                prod = work.tile([P, 2, S], F32, name="prod", tag="late", bufs=1, align_bytes=64)
+            else:
+                prod = work.tile([P, 2, S], F32, name="prod", align_bytes=64)
+            dot = dots[:, (PACK - 1 - t) * S : (PACK - t) * S]
+            if t in DOT_V:
+                for w in range(2):
+                    nc.vector.tensor_tensor(prod[:, w, :], bond[:, w, :], bond[:, 2 + w, :], ALU.mult)
+                nc.vector.tensor_tensor(dot, prod[:, 0, :], prod[:, 1, :], ALU.add)
+            else:
+                if SPLITM:
+                    for w in range(2):
+                        nc.gpsimd.tensor_tensor(prod[:, w, :], bond[:, w, :], bond[:, 2 + w, :], ALU.mult)
+                else:
+                    nc.gpsimd.tensor_tensor(prod[:], bond[:, 0:2, :], bond[:, 2:4, :], ALU.mult)
+                nc.gpsimd.tensor_tensor(dot, prod[:, 0, :], prod[:, 1, :], ALU.add)
+
+        def make_squares(t):
+            bond = bonds[t]
+            sq = work.tile([P, 2, S], F32, name="sq", align_bytes=64)
+            if t in SQ_G:
+                nc.scalar.activation(sq[:, 0, :], bond[:, 0, :], ACT.Square)
+                nc.gpsimd.tensor_tensor(sq[:, 1, :], bond[:, 1, :], bond[:, 1, :], ALU.mult)
+            else:
+                nc.scalar.activation(sq[:], bond[:, 0:2, :], ACT.Square)
+            scaled = work.tile([P, S], F32, name="scaled", align_bytes=64)
+            if t in U_S:
+                nc.scalar.activation(scaled[:], sq[:, 0, :], ACT.Copy, scale=vir_unit[:, t : t + 1])
+            else:
+                nc.gpsimd.tensor_scalar(scaled[:], sq[:, 0, :], vir_unit[:, t : t + 1], 0.0, ALU.mult, ALU.add)
+            squares[t], scaleds[t] = sq, scaled
+
+        def make_virial(t):
+            sq = squares[t]
+            if t in VIR_L0:
+                if t == HOLD[0]:
+                    r2 = work.tile([P, S], F32, name="r2", tag="late", bufs=1, align_bytes=64)
+                else:
+                    r2 = work.tile([P, S], F32, name="r2", align_bytes=64)
+                denom = work.tile([P, S], F32, name="denom", align_bytes=64)
+                soft = work.tile([P, S], F32, name="soft", align_bytes=64)
+                vir = work.tile([P, S], F32, name="vir_t", align_bytes=64)
+                nc.vector.tensor_tensor(r2[:], sq[:, 0, :], sq[:, 1, :], ALU.add)
+                nc.scalar.activation(denom[:], r2[:], ACT.Square, bias=40.0 * Z_SCALE, scale=Z_SCALE)
+                nc.scalar.activation(soft[:], denom[:], ACT.Abs_reciprocal_sqrt)
+                nc.vector.scalar_tensor_tensor(
+                    vir[:], soft[:], 1.0 / (36.0 * Z_SCALE), scaleds[t][:], ALU.subtract, ALU.mult
+                )
+                virs[t] = vir
+                return
+            r2_t = psum.tile([P, S], F32, name="r2_t", bufs=1)
+            turn(r2_t, [sq[:, 0, :], sq[:, 1, :]])
+            scaled_t = psum.tile([P, S], F32, name="scaled_t", bufs=1)
+            turn(scaled_t, [scaleds[t]])
+            denom = work.tile([P, S], F32, name="denom", align_bytes=64)
+            soft = work.tile([P, S], F32, name="soft", align_bytes=64)
+            vir_t = work.tile([P, S], F32, name="vir_t", align_bytes=64)
+            nc.scalar.activation(denom[:], r2_t[:], ACT.Square, bias=40.0 * Z_SCALE, scale=Z_SCALE)
+            nc.scalar.activation(soft[:], denom[:], ACT.Abs_reciprocal_sqrt)
+            nc.vector.scalar_tensor_tensor(
+                vir_t[:], soft[:], 1.0 / (36.0 * Z_SCALE), scaled_t[:], ALU.subtract, ALU.mult
+            )
+            vir = psum.tile([P, S], F32, name="vir")
+            turn(vir, [vir_t])
+            virs[t] = vir
+
+        def make_hidden(t):
+            bend = work.tile([P, S], F32, name="bend", align_bytes=64)
+            window = dots[:, (PACK - 1 - t) * S : (PACK + 1 - t) * S]
+            if t == PACK - 1:
+                for h in range(2):
+                    cols = slice(h * HALF, (h + 1) * HALF)
+                    gather(h == 0, bend[:, cols], window, nxt_sb[:, h * HALF // 16 : (h + 1) * HALF // 16])
+            else:
+                gather(t in BEND_V, bend[:], window, nxt_sb[:])
+                nc.vector.scalar_tensor_tensor(
+                    hid[:, t, :], bend[:], bend_unit[:, t : t + 1], virs[t][:], ALU.mult, ALU.add
+                )
+            bends[t] = bend
+
+        stages = {"b": make_bonds, "d": make_dot, "s": make_squares, "v": make_virial, "h": make_hidden}
+        for step in ORDER.split():
+            stages[step[0]](int(step[1]))
+
+        bend, vir = bends[PACK - 1], virs[PACK - 1]
+        t = PACK - 1
+        out_rows = out.rearrange("(b p) j -> p b j", p=P)
+        for c in range(S // OUT_COLS):
+            cols = slice(c * OUT_COLS, (c + 1) * OUT_COLS)
+            nc.vector.scalar_tensor_tensor(
+                hid[:, t, cols], bend[:, cols], bend_unit[:, t : t + 1], vir[:, cols], ALU.mult, ALU.add
+            )
+            woven = work.tile([P, OUT_COLS, PACK], BF16, name="woven", align_bytes=64)
+            dst = woven[:].rearrange("p (c i) t -> p c t i", i=4)
+            src = hid[:, :, cols].rearrange("p t (c i) -> p c t i", i=4)
+            if c not in IL_S:
+                nc.vector.tensor_copy(dst, src)
+            else:
+                nc.scalar.copy(dst, src)
+            codes = work.tile([P, OUT_COLS], U32, name="codes", align_bytes=64)
+            scales = work.tile([P, OUT_COLS], U8, name="scales", align_bytes=64)
+            nc.vector.quantize_mx(
+                out=codes[:].bitcast(FP8X4), scales=scales[:], in_=woven[:].rearrange("p c t -> p (c t)")
+            )
+            acc = psum.tile([P, S], F32, name="acc", tag="pos%d" % (c % 2))
+            for b in range(N // P):
+                nc.tensor.matmul_mx(
+                    out=acc[:, b * OUT_COLS : (b + 1) * OUT_COLS],
+                    lhsT=w3w[:, 2 * b * P : 2 * (b + 1) * P].bitcast(FP4X4),
+                    lhsT_scale=ws[:, 2 * H + b * P : 2 * H + (b + 1) * P],
+                    rhs=codes[:].bitcast(FP8X4),
+                    rhs_scale=scales[:],
+                    start=True,
+                    stop=True,
+                )
+            res = work.tile([P, N // P, OUT_COLS], F32, name="res", align_bytes=64)
+            nc.scalar.copy(res[:].rearrange("p b j -> p (b j)"), acc[:, 0 : (N // P) * OUT_COLS])
+            nc.sync.dma_start(out_rows[:, :, cols], res[:])

@@ -22,18 +22,22 @@ PACK = 4
 HALF = S // 2
 OUT_COLS = 128
 Z_SCALE = 1.140625 / 40.0
-EVAC_S = {(0, 0, 0), (0, 1, 0), (0, 0, HALF)}
-U_S = {3}
-VIR_L0 = {3}
-HOLD = (-1, -1)
-XFIRST = False
-GATHER_V = {(0,1),(0,3),(1,1),(2,1),(3,1)}
-DOT_V = {3}
-SQ_G = {0,1}
-BEND_V = {0}
-SPLITM = False
-IL_S = {1, 3}
-ORDER = "b0 d0 s0 b1 d1 v0 s1 h0 b2 d2 v1 s2 h1 b3 s3 v2 d3 v3 h2 h3"
+EVAC_S = {(t, 0, 0) for t in range(4)}
+GATHER_V = {(t, 2) for t in range(4)} | {(0, 0), (1, 0)}
+DOT_G = set()
+SQ_G = set()
+BEND_V = set()
+WARM = False
+HOLD = -1
+HALVES = False
+SPLIT_LAST = True
+SUB_SB = {0,1,2,3}
+POS_BUFS = 2
+R2_BUFS = 2
+QA = "sync"
+QB = "sync"
+QC = "sync"
+ORDER = "b0 n0 N0 s0 b1 n1 N1 s1 b2 n2 N2 s2 b3 n3 N3 s3 p0 P0 d0 v0 p1 P1 d1 v1 p2 P2 d2 v2 p3 P3 d3 v3 a0 h0 a1 h1 a2 h2 a3 h3"
 
 
 def tile_picked_ypolym_vir_p_kernel(
@@ -68,16 +72,14 @@ def tile_picked_ypolym_vir_p_kernel(
             for q in range(4):
                 queue.dma_start(dst[32 * q : 32 * q + 4, :].bitcast(I32), src[0, 4 * q : 4 * q + 4, :].bitcast(I32))
 
+        queues = {"sync": nc.sync, "scalar": nc.scalar, "gpsimd": nc.gpsimd}
         nc.sync.dma_start(offs_sb[:], offs)
-        if XFIRST:
-            nc.sync.dma_start(xw[:].bitcast(I32), x_words[0].rearrange("p n t -> p (n t)").bitcast(I32))
-        nc.sync.dma_start(ww[:, 0, :].bitcast(I32), w1_words[0].bitcast(I32))
-        nc.sync.dma_start(ww[:, 1, :].bitcast(I32), w2_words[0].bitcast(I32))
-        if not XFIRST:
-            nc.sync.dma_start(xw[:].bitcast(I32), x_words[0].rearrange("p n t -> p (n t)").bitcast(I32))
+        queues[QA].dma_start(ww[:, 0, :].bitcast(I32), w1_words[0].bitcast(I32))
+        queues[QA].dma_start(ww[:, 1, :].bitcast(I32), w2_words[0].bitcast(I32))
+        nc.sync.dma_start(xw[:].bitcast(I32), x_words[0].rearrange("p n t -> p (n t)").bitcast(I32))
         load_scales(nc.sync, xs, x_scales)
-        load_scales(nc.sync, ws[:, 0:H], w1_scales)
-        load_scales(nc.sync, ws[:, H : 2 * H], w2_scales)
+        load_scales(queues[QB], ws[:, 0:H], w1_scales)
+        load_scales(queues[QC], ws[:, H : 2 * H], w2_scales)
         nc.sync.dma_start(nxt_sb[:], nxt)
         nc.sync.dma_start(prv_sb[:], prv)
         nc.sync.dma_start(unit_sb[:], unit.rearrange("(p t) o -> p (t o)", t=PACK))
@@ -100,17 +102,23 @@ def tile_picked_ypolym_vir_p_kernel(
             nc.vector.tensor_copy(xg[:, cols], xw[:].indirect(part))
             nc.vector.tensor_copy(sg[:, cols], xs[:].indirect(part))
             if h == 0:
-                for w in range(2):
-                    nc.vector.tensor_copy(
-                        sd[:, w, :, :], ws[:, w * H : (w + 1) * H].rearrange("p (m t) -> p t m", t=PACK)
-                    )
+                nc.vector.tensor_copy(
+                    sd[:], ws[:, 0 : 2 * H].rearrange("p (w m t) -> p w t m", w=2, t=PACK)
+                )
 
         vir_unit = held.tile([P, PACK], F32, name="vir_unit")
         bend_unit = held.tile([P, PACK], F32, name="bend_unit")
         nc.gpsimd.tensor_scalar(vir_unit[:], unit_sb[:], -360.0 * Z_SCALE, 0.0, ALU.mult, ALU.add)
         nc.gpsimd.tensor_scalar(bend_unit[:], unit_sb[:], -0.3, 0.0, ALU.mult, ALU.add)
 
-        hid = held.tile([P, PACK, S], F32, name="hid", align_bytes=64)
+        shift = held.tile([P, 1], F32, name="shift")
+        nc.gpsimd.memset(shift[:], 1.0)
+        if WARM:
+            warm = held.tile([P, 1], F32, name="warm")
+            nc.scalar.activation(warm[:], shift[:], ACT.Abs_reciprocal_sqrt)
+        nc.gpsimd.tensor_scalar(shift[:], shift[:], -1.0 / (36.0 * Z_SCALE), 0.0, ALU.mult, ALU.add)
+        vir = held.tile([P, PACK, S], F32, name="vir", align_bytes=64)
+        late = {}
 
         def gather(on_vector, dst, window, offsets):
             if on_vector:
@@ -123,17 +131,17 @@ def tile_picked_ypolym_vir_p_kernel(
                 cols = slice(c * P, (c + 1) * P)
                 for n, src in enumerate(srcs):
                     nc.tensor.matmul(
-                        dst[:, cols], lhsT=src[:, cols], rhs=ident[:], start=(n == 0), stop=(n == len(srcs) - 1),
+                        dst[:, cols], lhsT=src[:, cols] if src.shape[1] == S else src, rhs=ident[:], start=(n == 0), stop=(n == len(srcs) - 1),
                         is_transpose=True,
                     )
 
-        bonds, squares, scaleds, virs, bends = {}, {}, {}, {}, {}
+        bonds, squares, poss, bases, gots, stiffs = {}, {}, {}, {}, {}, {}
 
         def make_bonds(t):
             first = t == 0
             base = [(2 * (PACK - 1 - t) + 1 - w) * S for w in range(2)]
-            pos = [psum.tile([P, S], F32, name="acc", tag="pos%d" % w) for w in range(2)]
-            widths = [HALF, HALF] if first else [S]
+            pos = [psum.tile([P, S], F32, name="acc", tag="pos%d" % w, bufs=POS_BUFS) for w in range(2)]
+            widths = [HALF, HALF] if first and HALVES else [S]
             c0 = 0
             for width in widths:
                 cols = slice(c0, c0 + width)
@@ -153,33 +161,38 @@ def tile_picked_ypolym_vir_p_kernel(
                     else:
                         nc.vector.tensor_copy(dst, pos[w][:, cols])
                 c0 += width
-            got = work.tile([P, 4, S], F32, name="got", align_bytes=64)
-            bond = work.tile([P, 4, S], F32, name="bond", align_bytes=64)
-            for n, offsets in enumerate((nxt_sb, prv_sb)):
-                for w in range(2):
-                    window = coords[:, base[w] : base[w] + 2 * S]
-                    gather((t, 2 * n + w) in GATHER_V, got[:, 2 * n + w, :], window, offsets[:])
-                    nc.vector.tensor_tensor(bond[:, 2 * n + w, :], got[:, 2 * n + w, :], pos[w][:], ALU.subtract)
-            bonds[t] = bond
+            poss[t], bases[t] = pos, base
+            gots[t] = work.tile([P, 4, S], F32, name="got", align_bytes=64)
+            bonds[t] = work.tile([P, 4, S], F32, name="bond", align_bytes=64)
+
+        def fetch(t, n):
+            for w in range(2):
+                window = coords[:, bases[t][w] : bases[t][w] + 2 * S]
+                gather((t, 2 * n + w) in GATHER_V, gots[t][:, 2 * n + w, :], window, (nxt_sb, prv_sb)[n][:])
+
+        def subtract(t, n):
+            for w in range(2):
+                own = coords[:, bases[t][w] : bases[t][w] + S] if t in SUB_SB else poss[t][w][:]
+                nc.vector.tensor_tensor(bonds[t][:, 2 * n + w, :], gots[t][:, 2 * n + w, :], own, ALU.subtract)
 
         def make_dot(t):
             bond = bonds[t]
-            if t == HOLD[1]:
-                prod = work.tile([P, 2, S], F32, name="prod", tag="late", bufs=1, align_bytes=64)
-            else:
-                prod = work.tile([P, 2, S], F32, name="prod", align_bytes=64)
+            prod = work.tile([P, 2, S], F32, name="prod", align_bytes=64)
             dot = dots[:, (PACK - 1 - t) * S : (PACK - t) * S]
-            if t in DOT_V:
-                for w in range(2):
-                    nc.vector.tensor_tensor(prod[:, w, :], bond[:, w, :], bond[:, 2 + w, :], ALU.mult)
-                nc.vector.tensor_tensor(dot, prod[:, 0, :], prod[:, 1, :], ALU.add)
-            else:
-                if SPLITM:
-                    for w in range(2):
-                        nc.gpsimd.tensor_tensor(prod[:, w, :], bond[:, w, :], bond[:, 2 + w, :], ALU.mult)
+            if t in DOT_G:
+                nc.gpsimd.tensor_tensor(prod[:], bond[:, 0:2, :], bond[:, 2:4, :], ALU.mult)
+                if t == HOLD:
+                    raw = held.tile([P, S], F32, name="raw", tag="bend", align_bytes=64)
                 else:
-                    nc.gpsimd.tensor_tensor(prod[:], bond[:, 0:2, :], bond[:, 2:4, :], ALU.mult)
-                nc.gpsimd.tensor_tensor(dot, prod[:, 0, :], prod[:, 1, :], ALU.add)
+                    raw = work.tile([P, S], F32, name="raw", align_bytes=64)
+                nc.gpsimd.tensor_tensor(raw[:], prod[:, 0, :], prod[:, 1, :], ALU.add)
+                nc.gpsimd.tensor_scalar(dot, raw[:], bend_unit[:, t : t + 1], 0.0, ALU.mult, ALU.add)
+            else:
+                for w in range(2):
+                    nc.vector.scalar_tensor_tensor(
+                        prod[:, w, :], bond[:, w, :], bend_unit[:, t : t + 1], bond[:, 2 + w, :], ALU.mult, ALU.mult
+                    )
+                nc.vector.tensor_tensor(dot, prod[:, 0, :], prod[:, 1, :], ALU.add)
 
         def make_squares(t):
             bond = bonds[t]
@@ -189,86 +202,60 @@ def tile_picked_ypolym_vir_p_kernel(
                 nc.gpsimd.tensor_tensor(sq[:, 1, :], bond[:, 1, :], bond[:, 1, :], ALU.mult)
             else:
                 nc.scalar.activation(sq[:], bond[:, 0:2, :], ACT.Square)
-            scaled = work.tile([P, S], F32, name="scaled", align_bytes=64)
-            if t in U_S:
-                nc.scalar.activation(scaled[:], sq[:, 0, :], ACT.Copy, scale=vir_unit[:, t : t + 1])
-            else:
-                nc.gpsimd.tensor_scalar(scaled[:], sq[:, 0, :], vir_unit[:, t : t + 1], 0.0, ALU.mult, ALU.add)
-            squares[t], scaleds[t] = sq, scaled
+            squares[t] = sq
 
         def make_virial(t):
             sq = squares[t]
-            if t in VIR_L0:
-                if t == HOLD[0]:
-                    r2 = work.tile([P, S], F32, name="r2", tag="late", bufs=1, align_bytes=64)
-                else:
-                    r2 = work.tile([P, S], F32, name="r2", align_bytes=64)
-                denom = work.tile([P, S], F32, name="denom", align_bytes=64)
-                soft = work.tile([P, S], F32, name="soft", align_bytes=64)
-                vir = work.tile([P, S], F32, name="vir_t", align_bytes=64)
-                nc.vector.tensor_tensor(r2[:], sq[:, 0, :], sq[:, 1, :], ALU.add)
-                nc.scalar.activation(denom[:], r2[:], ACT.Square, bias=40.0 * Z_SCALE, scale=Z_SCALE)
-                nc.scalar.activation(soft[:], denom[:], ACT.Abs_reciprocal_sqrt)
-                nc.vector.scalar_tensor_tensor(
-                    vir[:], soft[:], 1.0 / (36.0 * Z_SCALE), scaleds[t][:], ALU.subtract, ALU.mult
-                )
-                virs[t] = vir
-                return
-            r2_t = psum.tile([P, S], F32, name="r2_t", bufs=1)
+            r2_t = psum.tile([P, S], F32, name="r2_t", bufs=R2_BUFS)
             turn(r2_t, [sq[:, 0, :], sq[:, 1, :]])
-            scaled_t = psum.tile([P, S], F32, name="scaled_t", bufs=1)
-            turn(scaled_t, [scaleds[t]])
             denom = work.tile([P, S], F32, name="denom", align_bytes=64)
             soft = work.tile([P, S], F32, name="soft", align_bytes=64)
-            vir_t = work.tile([P, S], F32, name="vir_t", align_bytes=64)
             nc.scalar.activation(denom[:], r2_t[:], ACT.Square, bias=40.0 * Z_SCALE, scale=Z_SCALE)
             nc.scalar.activation(soft[:], denom[:], ACT.Abs_reciprocal_sqrt)
+            stiff = psum.tile([P, S], F32, name="stiff", bufs=8 - 2 * POS_BUFS - R2_BUFS)
+            turn(stiff, [shift[:].to_broadcast([P, P]), soft[:]])
+            stiffs[t] = stiff
+
+        def finish_virial(t):
             nc.vector.scalar_tensor_tensor(
-                vir_t[:], soft[:], 1.0 / (36.0 * Z_SCALE), scaled_t[:], ALU.subtract, ALU.mult
+                vir[:, t, :], stiffs[t][:], vir_unit[:, t : t + 1], squares[t][:, 0, :], ALU.mult, ALU.mult
             )
-            vir = psum.tile([P, S], F32, name="vir")
-            turn(vir, [vir_t])
-            virs[t] = vir
 
         def make_hidden(t):
-            bend = work.tile([P, S], F32, name="bend", align_bytes=64)
+            if "bend" not in late:
+                late["bend"] = held.tile([P, PACK, S], F32, name="bend", tag="bend", align_bytes=64)
+            bend = late["bend"]
             window = dots[:, (PACK - 1 - t) * S : (PACK + 1 - t) * S]
-            if t == PACK - 1:
+            if t == PACK - 1 and SPLIT_LAST:
                 for h in range(2):
                     cols = slice(h * HALF, (h + 1) * HALF)
-                    gather(h == 0, bend[:, cols], window, nxt_sb[:, h * HALF // 16 : (h + 1) * HALF // 16])
+                    gather(h == 0, bend[:, t, cols], window, nxt_sb[:, h * HALF // 16 : (h + 1) * HALF // 16])
             else:
-                gather(t in BEND_V, bend[:], window, nxt_sb[:])
-                nc.vector.scalar_tensor_tensor(
-                    hid[:, t, :], bend[:], bend_unit[:, t : t + 1], virs[t][:], ALU.mult, ALU.add
-                )
-            bends[t] = bend
+                gather(t in BEND_V, bend[:, t, :], window, nxt_sb[:])
 
-        stages = {"b": make_bonds, "d": make_dot, "s": make_squares, "v": make_virial, "h": make_hidden}
+        stages = {"b": make_bonds, "d": make_dot, "s": make_squares, "v": make_virial, "h": make_hidden,
+                  "n": lambda t: fetch(t, 0), "p": lambda t: fetch(t, 1), "N": lambda t: subtract(t, 0),
+                  "P": lambda t: subtract(t, 1), "a": finish_virial}
         for step in ORDER.split():
             stages[step[0]](int(step[1]))
 
-        bend, vir = bends[PACK - 1], virs[PACK - 1]
-        t = PACK - 1
+        bend = late["bend"]
         out_rows = out.rearrange("(b p) j -> p b j", p=P)
         for c in range(S // OUT_COLS):
             cols = slice(c * OUT_COLS, (c + 1) * OUT_COLS)
-            nc.vector.scalar_tensor_tensor(
-                hid[:, t, cols], bend[:, cols], bend_unit[:, t : t + 1], vir[:, cols], ALU.mult, ALU.add
-            )
             woven = work.tile([P, OUT_COLS, PACK], BF16, name="woven", align_bytes=64)
-            dst = woven[:].rearrange("p (c i) t -> p c t i", i=4)
-            src = hid[:, :, cols].rearrange("p t (c i) -> p c t i", i=4)
-            if c not in IL_S:
-                nc.vector.tensor_copy(dst, src)
-            else:
-                nc.scalar.copy(dst, src)
+            nc.vector.tensor_tensor(
+                woven[:].rearrange("p (c i) t -> p c t i", i=4),
+                vir[:, :, cols].rearrange("p t (c i) -> p c t i", i=4),
+                bend[:, :, cols].rearrange("p t (c i) -> p c t i", i=4),
+                ALU.add,
+            )
             codes = work.tile([P, OUT_COLS], U32, name="codes", align_bytes=64)
             scales = work.tile([P, OUT_COLS], U8, name="scales", align_bytes=64)
             nc.vector.quantize_mx(
                 out=codes[:].bitcast(FP8X4), scales=scales[:], in_=woven[:].rearrange("p c t -> p (c t)")
             )
-            acc = psum.tile([P, S], F32, name="acc", tag="pos%d" % (c % 2))
+            acc = psum.tile([P, S], F32, name="acc", tag="pos%d" % (c % 2), bufs=POS_BUFS)
             for b in range(N // P):
                 nc.tensor.matmul_mx(
                     out=acc[:, b * OUT_COLS : (b + 1) * OUT_COLS],

@@ -23,21 +23,25 @@ HALF = S // 2
 OUT_COLS = 128
 Z_SCALE = 1.140625 / 40.0
 EVAC_S = {(t, 0, 0) for t in range(4)}
-GATHER_V = {(t, 2) for t in range(4)} | {(0, 0), (1, 0)}
+GATHER_V = {(t, w) for t in range(4) for w in range(2)}
 DOT_G = set()
 SQ_G = set()
 BEND_V = set()
 WARM = False
+PSUB_G = {0, 1, 2, 3}
+TAILW = 256
+TAIL_A = {0, 1, 2, 3}
+EARLY = 2
 HOLD = -1
 HALVES = False
 SPLIT_LAST = True
-SUB_SB = {0,1,2,3}
+SUB_SB = {(t, 1) for t in range(4)}
 POS_BUFS = 2
 R2_BUFS = 2
 QA = "sync"
 QB = "sync"
 QC = "sync"
-ORDER = "b0 n0 N0 s0 b1 n1 N1 s1 b2 n2 N2 s2 b3 n3 N3 s3 p0 P0 d0 v0 p1 P1 d1 v1 p2 P2 d2 v2 p3 P3 d3 v3 a0 h0 a1 h1 a2 h2 a3 h3"
+ORDER = "b0 n0 N0 p0 P0 b1 n1 N1 p1 P1 b2 n2 N2 p2 P2 b3 n3 N3 p3 P3 s0 v0 d0 s1 v1 d1 s2 v2 d2 s3 v3 d3"
 
 
 def tile_picked_ypolym_vir_p_kernel(
@@ -96,15 +100,11 @@ def tile_picked_ypolym_vir_p_kernel(
 
         xg = held.tile([P, S], U32, name="xg", align_bytes=64)
         sg = held.tile([P, S], U8, name="sg", align_bytes=64)
-        for h in range(2):
-            cols = slice(h * HALF, (h + 1) * HALF)
-            part = offs_sb[:, h * HALF // 16 : (h + 1) * HALF // 16]
-            nc.vector.tensor_copy(xg[:, cols], xw[:].indirect(part))
-            nc.vector.tensor_copy(sg[:, cols], xs[:].indirect(part))
-            if h == 0:
-                nc.vector.tensor_copy(
-                    sd[:], ws[:, 0 : 2 * H].rearrange("p (w m t) -> p w t m", w=2, t=PACK)
-                )
+        nc.vector.tensor_copy(xg[:], xw[:].indirect(offs_sb[:]))
+        nc.vector.tensor_copy(sg[:], xs[:].indirect(offs_sb[:]))
+        dealt = ws[:, 0 : 2 * H].rearrange("p (w m t) -> p w t m", w=2, t=PACK)
+        nc.vector.tensor_copy(sd[:, :, 0:1, :], dealt[:, :, 0:1, :])
+        nc.vector.tensor_copy(sd[:, :, 1:PACK, :], dealt[:, :, 1:PACK, :])
 
         vir_unit = held.tile([P, PACK], F32, name="vir_unit")
         bend_unit = held.tile([P, PACK], F32, name="bend_unit")
@@ -171,8 +171,13 @@ def tile_picked_ypolym_vir_p_kernel(
                 gather((t, 2 * n + w) in GATHER_V, gots[t][:, 2 * n + w, :], window, (nxt_sb, prv_sb)[n][:])
 
         def subtract(t, n):
+            if n == 1 and t in PSUB_G:
+                for w in range(2):
+                    own = coords[:, bases[t][w] : bases[t][w] + S]
+                    nc.gpsimd.tensor_tensor(bonds[t][:, 2 + w, :], gots[t][:, 2 + w, :], own, ALU.subtract)
+                return
             for w in range(2):
-                own = coords[:, bases[t][w] : bases[t][w] + S] if t in SUB_SB else poss[t][w][:]
+                own = coords[:, bases[t][w] : bases[t][w] + S] if (t, n) in SUB_SB else poss[t][w][:]
                 nc.vector.tensor_tensor(bonds[t][:, 2 * n + w, :], gots[t][:, 2 * n + w, :], own, ALU.subtract)
 
         def make_dot(t):
@@ -212,13 +217,16 @@ def tile_picked_ypolym_vir_p_kernel(
             soft = work.tile([P, S], F32, name="soft", align_bytes=64)
             nc.scalar.activation(denom[:], r2_t[:], ACT.Square, bias=40.0 * Z_SCALE, scale=Z_SCALE)
             nc.scalar.activation(soft[:], denom[:], ACT.Abs_reciprocal_sqrt)
-            stiff = psum.tile([P, S], F32, name="stiff", bufs=8 - 2 * POS_BUFS - R2_BUFS)
+            if t < EARLY:
+                stiff = psum.tile([P, S], F32, name="stiff", bufs=2)
+            else:
+                stiff = psum.tile([P, S], F32, name="stiff", tag="pos%d" % (t % 2), bufs=POS_BUFS)
             turn(stiff, [shift[:].to_broadcast([P, P]), soft[:]])
             stiffs[t] = stiff
 
-        def finish_virial(t):
+        def finish_virial(t, cols=slice(0, S)):
             nc.vector.scalar_tensor_tensor(
-                vir[:, t, :], stiffs[t][:], vir_unit[:, t : t + 1], squares[t][:, 0, :], ALU.mult, ALU.mult
+                vir[:, t, cols], stiffs[t][:, cols], vir_unit[:, t : t + 1], squares[t][:, 0, cols], ALU.mult, ALU.mult
             )
 
         def make_hidden(t):
@@ -239,10 +247,19 @@ def tile_picked_ypolym_vir_p_kernel(
         for step in ORDER.split():
             stages[step[0]](int(step[1]))
 
+        if TAILW:
+            late["bend"] = held.tile([P, PACK, S], F32, name="bend", tag="bend", align_bytes=64)
         bend = late["bend"]
         out_rows = out.rearrange("(b p) j -> p b j", p=P)
         for c in range(S // OUT_COLS):
             cols = slice(c * OUT_COLS, (c + 1) * OUT_COLS)
+            if TAILW and (c * OUT_COLS) % TAILW == 0:
+                wide = slice(c * OUT_COLS, c * OUT_COLS + TAILW)
+                for t in range(PACK):
+                    window = dots[:, (PACK - 1 - t) * S : (PACK + 1 - t) * S]
+                    gather((t, c) in BEND_V, bend[:, t, wide], window, nxt_sb[:, wide.start // 16 : wide.stop // 16])
+                    if t in TAIL_A:
+                        finish_virial(t, wide)
             woven = work.tile([P, OUT_COLS, PACK], BF16, name="woven", align_bytes=64)
             nc.vector.tensor_tensor(
                 woven[:].rearrange("p (c i) t -> p c t i", i=4),
@@ -255,7 +272,7 @@ def tile_picked_ypolym_vir_p_kernel(
             nc.vector.quantize_mx(
                 out=codes[:].bitcast(FP8X4), scales=scales[:], in_=woven[:].rearrange("p c t -> p (c t)")
             )
-            acc = psum.tile([P, S], F32, name="acc", tag="pos%d" % (c % 2), bufs=POS_BUFS)
+            acc = psum.tile([P, S], F32, name="total", tag="r2_t" if EARLY else "total", bufs=2)
             for b in range(N // P):
                 nc.tensor.matmul_mx(
                     out=acc[:, b * OUT_COLS : (b + 1) * OUT_COLS],

@@ -27,7 +27,7 @@ GATHER_V = {(t, w) for t in range(4) for w in range(2)}
 DOT_G = set()
 SQ_G = set()
 BEND_V = set()
-WARM = False
+WARM = True
 PSUB_G = {0, 1, 2, 3}
 TAILW = 256
 TAIL_A = {0, 1, 2, 3}

@@ -19,92 +19,77 @@ ACT = mybir.ActivationFunctionType
 
 P = 128
 PACK = 4
+GROUP = 16
+X, Y = 0, 1
 HALF = S // 2
 OUT_COLS = 128
+LINE = 4
 Z_SCALE = 1.140625 / 40.0
-EVAC_S = {(t, 0, 0) for t in range(4)}
-GATHER_V = {(t, w) for t in range(4) for w in range(2)}
-DOT_G = set()
-SQ_G = set()
-BEND_V = set()
-WARM = True
-PSUB_G = {0, 1, 2, 3}
-TAILW = 256
-TAIL_A = {0, 1, 2, 3}
-EARLY = 2
-HOLD = -1
-HALVES = False
-SPLIT_LAST = True
-SUB_SB = {(t, 1) for t in range(4)}
-POS_BUFS = 2
-R2_BUFS = 2
-QA = "sync"
-QB = "sync"
-QC = "sync"
-ORDER = "b0 n0 N0 p0 P0 b1 n1 N1 p1 P1 b2 n2 N2 p2 P2 b3 n3 N3 p3 P3 s0 v0 d0 s1 v1 d1 s2 v2 d2 s3 v3 d3"
 
 
 def tile_picked_ypolym_vir_p_kernel(
     tc, x_words, x_scales, w1_words, w1_scales, w2_words, w2_scales, unit, w3_words, w3_scales, offs, nxt, prv, out
 ):
     nc = tc.nc
+    planes = range(PACK)
     with ExitStack() as ctx:
         held = ctx.enter_context(tc.tile_pool(name="held", bufs=1))
-        work = ctx.enter_context(tc.tile_pool(name="work", bufs=4))
+        work = ctx.enter_context(tc.tile_pool(name="work", bufs=PACK))
         psum = ctx.enter_context(tc.psum_pool(name="psum", bufs=2))
 
-        offs_sb = held.tile([P, S // 16], U16, name="offs_sb")
-        nxt_sb = held.tile([P, S // 16], U16, name="nxt_sb")
-        prv_sb = held.tile([P, S // 16], U16, name="prv_sb")
-        xw = held.tile([P, T], U32, name="xw", align_bytes=64)
-        xs = held.tile([P, T], U8, name="xs", align_bytes=64)
-        ww = held.tile([P, 2, 2 * H], U8, name="ww", align_bytes=64)
-        w3w = held.tile([P, 2 * N], U8, name="w3w", align_bytes=64)
-        ws = held.tile([P, 2 * H + N], U8, name="ws", align_bytes=64)
+        offs_sb = held.tile([P, S // GROUP], U16, name="offs_sb")
+        nxt_sb = held.tile([P, S // GROUP], U16, name="nxt_sb")
+        prv_sb = held.tile([P, S // GROUP], U16, name="prv_sb")
+        x_codes = held.tile([P, T], U32, name="x_codes", align_bytes=64)
+        x_bytes = held.tile([P, T], U8, name="x_bytes", align_bytes=64)
+        w12_codes = held.tile([P, 2, 2 * H], U8, name="w12_codes", align_bytes=64)
+        w3_codes = held.tile([P, 2 * N], U8, name="w3_codes", align_bytes=64)
+        w_bytes = held.tile([P, 2 * H + N], U8, name="w_bytes", align_bytes=64)
         unit_sb = held.tile([P, PACK], F32, name="unit_sb")
         coords = held.tile([P, (2 * PACK + 1) * S], F32, name="coords", align_bytes=64)
-        dots = held.tile([P, (PACK + 1) * S], F32, name="dots", align_bytes=64)
         ident = held.tile([P, P], F32, name="ident", align_bytes=64)
 
-        nc.vector.memset(xs[:].bitcast(I32), 0)
-        nc.vector.memset(ws[:].bitcast(I32), 0)
+        def first_column(t, w):
+            return (2 * (PACK - 1 - t) + 1 - w) * S
+
+        nc.vector.memset(x_bytes[:].bitcast(I32), 0)
+        nc.vector.memset(w_bytes[:].bitcast(I32), 0)
         nc.vector.memset(coords[:, 2 * PACK * S :], 0.0)
-        nc.vector.memset(dots[:, PACK * S :], 0.0)
         make_identity(nc, ident[:])
 
-        def load_scales(queue, dst, src):
+        def load_scale_rows(dst, src):
             for q in range(4):
-                queue.dma_start(dst[32 * q : 32 * q + 4, :].bitcast(I32), src[0, 4 * q : 4 * q + 4, :].bitcast(I32))
+                nc.sync.dma_start(dst[32 * q : 32 * q + 4, :].bitcast(I32), src[0, 4 * q : 4 * q + 4, :].bitcast(I32))
 
-        queues = {"sync": nc.sync, "scalar": nc.scalar, "gpsimd": nc.gpsimd}
         nc.sync.dma_start(offs_sb[:], offs)
-        queues[QA].dma_start(ww[:, 0, :].bitcast(I32), w1_words[0].bitcast(I32))
-        queues[QA].dma_start(ww[:, 1, :].bitcast(I32), w2_words[0].bitcast(I32))
-        nc.sync.dma_start(xw[:].bitcast(I32), x_words[0].rearrange("p n t -> p (n t)").bitcast(I32))
-        load_scales(nc.sync, xs, x_scales)
-        load_scales(queues[QB], ws[:, 0:H], w1_scales)
-        load_scales(queues[QC], ws[:, H : 2 * H], w2_scales)
+        nc.sync.dma_start(w12_codes[:, X, :].bitcast(I32), w1_words[0].bitcast(I32))
+        nc.sync.dma_start(w12_codes[:, Y, :].bitcast(I32), w2_words[0].bitcast(I32))
+        nc.sync.dma_start(x_codes[:].bitcast(I32), x_words[0].rearrange("p n t -> p (n t)").bitcast(I32))
+        load_scale_rows(x_bytes, x_scales)
+        load_scale_rows(w_bytes[:, 0:H], w1_scales)
+        load_scale_rows(w_bytes[:, H : 2 * H], w2_scales)
         nc.sync.dma_start(nxt_sb[:], nxt)
         nc.sync.dma_start(prv_sb[:], prv)
         nc.sync.dma_start(unit_sb[:], unit.rearrange("(p t) o -> p (t o)", t=PACK))
-        nc.sync.dma_start(w3w[:].bitcast(I32), w3_words[0].bitcast(I32))
-        load_scales(nc.sync, ws[:, 2 * H :], w3_scales)
+        nc.sync.dma_start(w3_codes[:].bitcast(I32), w3_words[0].bitcast(I32))
+        load_scale_rows(w_bytes[:, 2 * H :], w3_scales)
 
-        wd = held.tile([P, 2, PACK, 2 * P], U8, name="wd", align_bytes=64)
-        sd = held.tile([P, 2, PACK, P], U8, name="sd", align_bytes=64)
-        for w in range(2):
+        dealt_codes = held.tile([P, 2, PACK, 2 * P], U8, name="dealt_codes", align_bytes=64)
+        dealt_bytes = held.tile([P, 2, PACK, P], U8, name="dealt_bytes", align_bytes=64)
+        for w in (X, Y):
             nc.vector.tensor_copy(
-                wd[:, w, :, :].rearrange("p t (m b) -> p t m b", b=2),
-                ww[:, w, :].rearrange("p (m t b) -> p t m b", t=PACK, b=2),
+                dealt_codes[:, w, :, :].rearrange("p t (m b) -> p t m b", b=2),
+                w12_codes[:, w, :].rearrange("p (m t b) -> p t m b", t=PACK, b=2),
             )
 
-        xg = held.tile([P, S], U32, name="xg", align_bytes=64)
-        sg = held.tile([P, S], U8, name="sg", align_bytes=64)
-        nc.vector.tensor_copy(xg[:], xw[:].indirect(offs_sb[:]))
-        nc.vector.tensor_copy(sg[:], xs[:].indirect(offs_sb[:]))
-        dealt = ws[:, 0 : 2 * H].rearrange("p (w m t) -> p w t m", w=2, t=PACK)
-        nc.vector.tensor_copy(sd[:, :, 0:1, :], dealt[:, :, 0:1, :])
-        nc.vector.tensor_copy(sd[:, :, 1:PACK, :], dealt[:, :, 1:PACK, :])
+        picked_codes = held.tile([P, S], U32, name="picked_codes", align_bytes=64)
+        picked_bytes = held.tile([P, S], U8, name="picked_bytes", align_bytes=64)
+        nc.vector.tensor_copy(picked_codes[:], x_codes[:].indirect(offs_sb[:]))
+        nc.vector.tensor_copy(picked_bytes[:], x_bytes[:].indirect(offs_sb[:]))
+
+        by_plane = w_bytes[:, 0 : 2 * H].rearrange("p (w m t) -> p w t m", w=2, t=PACK)
+        nc.vector.tensor_copy(dealt_bytes[:, :, 0:1, :], by_plane[:, :, 0:1, :])
+        nc.vector.tensor_copy(dealt_bytes[:, :, 1:PACK, :], by_plane[:, :, 1:PACK, :])
 
         vir_unit = held.tile([P, PACK], F32, name="vir_unit")
         bend_unit = held.tile([P, PACK], F32, name="bend_unit")
@@ -113,176 +98,130 @@ def tile_picked_ypolym_vir_p_kernel(
 
         shift = held.tile([P, 1], F32, name="shift")
         nc.gpsimd.memset(shift[:], 1.0)
-        if WARM:
-            warm = held.tile([P, 1], F32, name="warm")
-            nc.scalar.activation(warm[:], shift[:], ACT.Abs_reciprocal_sqrt)
+        warm = held.tile([P, 1], F32, name="warm")
+        nc.scalar.activation(warm[:], shift[:], ACT.Abs_reciprocal_sqrt)
         nc.gpsimd.tensor_scalar(shift[:], shift[:], -1.0 / (36.0 * Z_SCALE), 0.0, ALU.mult, ALU.add)
-        vir = held.tile([P, PACK, S], F32, name="vir", align_bytes=64)
-        late = {}
 
-        def gather(on_vector, dst, window, offsets):
-            if on_vector:
-                nc.vector.tensor_copy(dst, window.indirect(offsets))
-            else:
-                nc.scalar.activation(dst, window.indirect(offsets), ACT.Copy)
-
-        def turn(dst, srcs):
+        def turn(dst, terms):
             for c in range(S // P):
                 cols = slice(c * P, (c + 1) * P)
-                for n, src in enumerate(srcs):
+                for n, term in enumerate(terms):
                     nc.tensor.matmul(
-                        dst[:, cols], lhsT=src[:, cols] if src.shape[1] == S else src, rhs=ident[:], start=(n == 0), stop=(n == len(srcs) - 1),
+                        dst[:, cols],
+                        lhsT=term(cols),
+                        rhs=ident[:],
+                        start=(n == 0),
+                        stop=(n == len(terms) - 1),
                         is_transpose=True,
                     )
 
-        bonds, squares, poss, bases, gots, stiffs = {}, {}, {}, {}, {}, {}
-
-        def make_bonds(t):
-            first = t == 0
-            base = [(2 * (PACK - 1 - t) + 1 - w) * S for w in range(2)]
-            pos = [psum.tile([P, S], F32, name="acc", tag="pos%d" % w, bufs=POS_BUFS) for w in range(2)]
-            widths = [HALF, HALF] if first and HALVES else [S]
-            c0 = 0
-            for width in widths:
-                cols = slice(c0, c0 + width)
-                for w in range(2):
-                    nc.tensor.matmul_mx(
-                        out=pos[w][:, cols],
-                        lhsT=wd[:, w, t, :].bitcast(FP4X4),
-                        lhsT_scale=sd[:, w, t, :],
-                        rhs=xg[:, cols].bitcast(FP8X4),
-                        rhs_scale=sg[:, cols],
-                        start=True,
-                        stop=True,
-                    )
-                    dst = coords[:, base[w] + c0 : base[w] + c0 + width]
-                    if (t, w, c0) in EVAC_S:
-                        nc.scalar.copy(dst, pos[w][:, cols])
-                    else:
-                        nc.vector.tensor_copy(dst, pos[w][:, cols])
-                c0 += width
-            poss[t], bases[t] = pos, base
-            gots[t] = work.tile([P, 4, S], F32, name="got", align_bytes=64)
-            bonds[t] = work.tile([P, 4, S], F32, name="bond", align_bytes=64)
-
-        def fetch(t, n):
-            for w in range(2):
-                window = coords[:, bases[t][w] : bases[t][w] + 2 * S]
-                gather((t, 2 * n + w) in GATHER_V, gots[t][:, 2 * n + w, :], window, (nxt_sb, prv_sb)[n][:])
-
-        def subtract(t, n):
-            if n == 1 and t in PSUB_G:
-                for w in range(2):
-                    own = coords[:, bases[t][w] : bases[t][w] + S]
-                    nc.gpsimd.tensor_tensor(bonds[t][:, 2 + w, :], gots[t][:, 2 + w, :], own, ALU.subtract)
-                return
-            for w in range(2):
-                own = coords[:, bases[t][w] : bases[t][w] + S] if (t, n) in SUB_SB else poss[t][w][:]
-                nc.vector.tensor_tensor(bonds[t][:, 2 * n + w, :], gots[t][:, 2 * n + w, :], own, ALU.subtract)
-
-        def make_dot(t):
-            bond = bonds[t]
-            prod = work.tile([P, 2, S], F32, name="prod", align_bytes=64)
-            dot = dots[:, (PACK - 1 - t) * S : (PACK - t) * S]
-            if t in DOT_G:
-                nc.gpsimd.tensor_tensor(prod[:], bond[:, 0:2, :], bond[:, 2:4, :], ALU.mult)
-                if t == HOLD:
-                    raw = held.tile([P, S], F32, name="raw", tag="bend", align_bytes=64)
-                else:
-                    raw = work.tile([P, S], F32, name="raw", align_bytes=64)
-                nc.gpsimd.tensor_tensor(raw[:], prod[:, 0, :], prod[:, 1, :], ALU.add)
-                nc.gpsimd.tensor_scalar(dot, raw[:], bend_unit[:, t : t + 1], 0.0, ALU.mult, ALU.add)
-            else:
-                for w in range(2):
-                    nc.vector.scalar_tensor_tensor(
-                        prod[:, w, :], bond[:, w, :], bend_unit[:, t : t + 1], bond[:, 2 + w, :], ALU.mult, ALU.mult
-                    )
-                nc.vector.tensor_tensor(dot, prod[:, 0, :], prod[:, 1, :], ALU.add)
-
-        def make_squares(t):
-            bond = bonds[t]
-            sq = work.tile([P, 2, S], F32, name="sq", align_bytes=64)
-            if t in SQ_G:
-                nc.scalar.activation(sq[:, 0, :], bond[:, 0, :], ACT.Square)
-                nc.gpsimd.tensor_tensor(sq[:, 1, :], bond[:, 1, :], bond[:, 1, :], ALU.mult)
-            else:
-                nc.scalar.activation(sq[:], bond[:, 0:2, :], ACT.Square)
-            squares[t] = sq
-
-        def make_virial(t):
-            sq = squares[t]
-            r2_t = psum.tile([P, S], F32, name="r2_t", bufs=R2_BUFS)
-            turn(r2_t, [sq[:, 0, :], sq[:, 1, :]])
-            denom = work.tile([P, S], F32, name="denom", align_bytes=64)
-            soft = work.tile([P, S], F32, name="soft", align_bytes=64)
-            nc.scalar.activation(denom[:], r2_t[:], ACT.Square, bias=40.0 * Z_SCALE, scale=Z_SCALE)
-            nc.scalar.activation(soft[:], denom[:], ACT.Abs_reciprocal_sqrt)
-            if t < EARLY:
-                stiff = psum.tile([P, S], F32, name="stiff", bufs=2)
-            else:
-                stiff = psum.tile([P, S], F32, name="stiff", tag="pos%d" % (t % 2), bufs=POS_BUFS)
-            turn(stiff, [shift[:].to_broadcast([P, P]), soft[:]])
-            stiffs[t] = stiff
-
-        def finish_virial(t, cols=slice(0, S)):
-            nc.vector.scalar_tensor_tensor(
-                vir[:, t, cols], stiffs[t][:, cols], vir_unit[:, t : t + 1], squares[t][:, 0, cols], ALU.mult, ALU.mult
-            )
-
-        def make_hidden(t):
-            if "bend" not in late:
-                late["bend"] = held.tile([P, PACK, S], F32, name="bend", tag="bend", align_bytes=64)
-            bend = late["bend"]
-            window = dots[:, (PACK - 1 - t) * S : (PACK + 1 - t) * S]
-            if t == PACK - 1 and SPLIT_LAST:
-                for h in range(2):
-                    cols = slice(h * HALF, (h + 1) * HALF)
-                    gather(h == 0, bend[:, t, cols], window, nxt_sb[:, h * HALF // 16 : (h + 1) * HALF // 16])
-            else:
-                gather(t in BEND_V, bend[:, t, :], window, nxt_sb[:])
-
-        stages = {"b": make_bonds, "d": make_dot, "s": make_squares, "v": make_virial, "h": make_hidden,
-                  "n": lambda t: fetch(t, 0), "p": lambda t: fetch(t, 1), "N": lambda t: subtract(t, 0),
-                  "P": lambda t: subtract(t, 1), "a": finish_virial}
-        for step in ORDER.split():
-            stages[step[0]](int(step[1]))
-
-        if TAILW:
-            late["bend"] = held.tile([P, PACK, S], F32, name="bend", tag="bend", align_bytes=64)
-        bend = late["bend"]
-        out_rows = out.rearrange("(b p) j -> p b j", p=P)
-        for c in range(S // OUT_COLS):
-            cols = slice(c * OUT_COLS, (c + 1) * OUT_COLS)
-            if TAILW and (c * OUT_COLS) % TAILW == 0:
-                wide = slice(c * OUT_COLS, c * OUT_COLS + TAILW)
-                for t in range(PACK):
-                    window = dots[:, (PACK - 1 - t) * S : (PACK + 1 - t) * S]
-                    gather((t, c) in BEND_V, bend[:, t, wide], window, nxt_sb[:, wide.start // 16 : wide.stop // 16])
-                    if t in TAIL_A:
-                        finish_virial(t, wide)
-            woven = work.tile([P, OUT_COLS, PACK], BF16, name="woven", align_bytes=64)
-            nc.vector.tensor_tensor(
-                woven[:].rearrange("p (c i) t -> p c t i", i=4),
-                vir[:, :, cols].rearrange("p t (c i) -> p c t i", i=4),
-                bend[:, :, cols].rearrange("p t (c i) -> p c t i", i=4),
-                ALU.add,
-            )
-            codes = work.tile([P, OUT_COLS], U32, name="codes", align_bytes=64)
-            scales = work.tile([P, OUT_COLS], U8, name="scales", align_bytes=64)
-            nc.vector.quantize_mx(
-                out=codes[:].bitcast(FP8X4), scales=scales[:], in_=woven[:].rearrange("p c t -> p (c t)")
-            )
-            acc = psum.tile([P, S], F32, name="total", tag="r2_t" if EARLY else "total", bufs=2)
-            for b in range(N // P):
+        bonds = []
+        for t in planes:
+            sums = [psum.tile([P, S], F32, name="sums", tag=("px", "py")[w]) for w in (X, Y)]
+            for w in (X, Y):
                 nc.tensor.matmul_mx(
-                    out=acc[:, b * OUT_COLS : (b + 1) * OUT_COLS],
-                    lhsT=w3w[:, 2 * b * P : 2 * (b + 1) * P].bitcast(FP4X4),
-                    lhsT_scale=ws[:, 2 * H + b * P : 2 * H + (b + 1) * P],
-                    rhs=codes[:].bitcast(FP8X4),
-                    rhs_scale=scales[:],
+                    out=sums[w][:],
+                    lhsT=dealt_codes[:, w, t, :].bitcast(FP4X4),
+                    lhsT_scale=dealt_bytes[:, w, t, :],
+                    rhs=picked_codes[:].bitcast(FP8X4),
+                    rhs_scale=picked_bytes[:],
                     start=True,
                     stop=True,
                 )
-            res = work.tile([P, N // P, OUT_COLS], F32, name="res", align_bytes=64)
-            nc.scalar.copy(res[:].rearrange("p b j -> p (b j)"), acc[:, 0 : (N // P) * OUT_COLS])
-            nc.sync.dma_start(out_rows[:, :, cols], res[:])
+                own = coords[:, first_column(t, w) : first_column(t, w) + S]
+                if w == X:
+                    nc.scalar.copy(own, sums[w][:])
+                else:
+                    nc.vector.tensor_copy(own, sums[w][:])
+            ahead = work.tile([P, 2, S], F32, name="ahead", align_bytes=64)
+            behind = work.tile([P, 2, S], F32, name="behind", align_bytes=64)
+            bond = work.tile([P, 4, S], F32, name="bond", align_bytes=64)
+            windows = [coords[:, first_column(t, w) : first_column(t, w) + 2 * S] for w in (X, Y)]
+            for w in (X, Y):
+                nc.vector.tensor_copy(ahead[:, w, :], windows[w].indirect(nxt_sb[:]))
+            for w in (X, Y):
+                nc.vector.tensor_tensor(bond[:, 1 - w, :], ahead[:, w, :], sums[w][:], ALU.subtract)
+            for w in (X, Y):
+                nc.scalar.activation(behind[:, 1 - w, :], windows[w].indirect(prv_sb[:]), ACT.Copy)
+            if t == 0:
+                for w in (X, Y):
+                    nc.gpsimd.tensor_tensor(bond[:, 3 - w, :], behind[:, 1 - w, :], windows[w][:, 0:S], ALU.subtract)
+            else:
+                both = windows[Y].rearrange("p (w s) -> p w s", w=2)
+                nc.gpsimd.tensor_tensor(bond[:, 2:4, :], behind[:], both, ALU.subtract)
+            bonds.append(bond)
+
+        squares, inverses = [], []
+        for t in planes:
+            square = work.tile([P, 2, S], F32, name="square", align_bytes=64)
+            nc.scalar.activation(square[:], bonds[t][:, 0:2, :], ACT.Square)
+            r2 = psum.tile([P, S], F32, name="r2", tag="turned")
+            turn(r2, [lambda cols: square[:, 0, cols], lambda cols: square[:, 1, cols]])
+            z2 = work.tile([P, S], F32, name="z2", align_bytes=64)
+            inverse = work.tile([P, S], F32, name="inverse", align_bytes=64)
+            nc.scalar.activation(z2[:], r2[:], ACT.Square, bias=40.0 * Z_SCALE, scale=Z_SCALE)
+            nc.scalar.activation(inverse[:], z2[:], ACT.Abs_reciprocal_sqrt)
+            squares.append(square)
+            inverses.append(inverse)
+
+        stiffs, dots = [], []
+        for t in planes:
+            stiff = psum.tile([P, S], F32, name="stiff", tag=("stiff", "stiff", "px", "py")[t])
+            turn(stiff, [lambda cols: shift[:].to_broadcast([P, P]), lambda cols: inverses[t][:, cols]])
+            bond, factor = bonds[t], bend_unit[:, t : t + 1]
+            terms = work.tile([P, 2, S], F32, name="terms", align_bytes=64)
+            dot = work.tile([P, S], F32, name="dot", align_bytes=64)
+            if t == 0:
+                plain_dot = held.tile([P, S], F32, name="plain_dot", align_bytes=64)
+                nc.gpsimd.tensor_tensor(terms[:], bond[:, 0:2, :], bond[:, 2:4, :], ALU.mult)
+                nc.gpsimd.tensor_tensor(plain_dot[:], terms[:, 0, :], terms[:, 1, :], ALU.add)
+                nc.gpsimd.tensor_scalar(dot[:], plain_dot[:], factor, 0.0, ALU.mult, ALU.add)
+            else:
+                for n in range(2):
+                    nc.vector.scalar_tensor_tensor(
+                        terms[:, n, :], bond[:, n, :], factor, bond[:, 2 + n, :], ALU.mult, ALU.mult
+                    )
+                nc.vector.tensor_tensor(dot[:], terms[:, 0, :], terms[:, 1, :], ALU.add)
+            stiffs.append(stiff)
+            dots.append(dot)
+
+        vir = held.tile([P, PACK, S], F32, name="vir", align_bytes=64)
+        bend = held.tile([P, PACK, S], F32, name="bend", align_bytes=64)
+        out_rows = out.rearrange("(b p) j -> p b j", p=P)
+        for first in range(0, S, HALF):
+            half = slice(first, first + HALF)
+            entries = nxt_sb[:, first // GROUP : (first + HALF) // GROUP]
+            for t in planes:
+                nc.scalar.activation(bend[:, t, half], dots[t][:].indirect(entries), ACT.Copy)
+                nc.vector.scalar_tensor_tensor(
+                    vir[:, t, half], stiffs[t][:, half], vir_unit[:, t : t + 1], squares[t][:, 1, half],
+                    ALU.mult, ALU.mult,
+                )
+            for c0 in range(first, first + HALF, OUT_COLS):
+                cols = slice(c0, c0 + OUT_COLS)
+                hid = work.tile([P, OUT_COLS, PACK], BF16, name="hid", align_bytes=64)
+                nc.vector.tensor_tensor(
+                    hid[:].rearrange("p (c i) t -> p c t i", i=LINE),
+                    vir[:, :, cols].rearrange("p t (c i) -> p c t i", i=LINE),
+                    bend[:, :, cols].rearrange("p t (c i) -> p c t i", i=LINE),
+                    ALU.add,
+                )
+                hid_codes = work.tile([P, OUT_COLS], U32, name="hid_codes", align_bytes=64)
+                hid_bytes = work.tile([P, OUT_COLS], U8, name="hid_bytes", align_bytes=64)
+                nc.vector.quantize_mx(
+                    out=hid_codes[:].bitcast(FP8X4), scales=hid_bytes[:], in_=hid[:].rearrange("p c t -> p (c t)")
+                )
+                total = psum.tile([P, S], F32, name="total", tag="turned")
+                for b in range(N // P):
+                    nc.tensor.matmul_mx(
+                        out=total[:, b * OUT_COLS : (b + 1) * OUT_COLS],
+                        lhsT=w3_codes[:, 2 * b * P : 2 * (b + 1) * P].bitcast(FP4X4),
+                        lhsT_scale=w_bytes[:, 2 * H + b * P : 2 * H + (b + 1) * P],
+                        rhs=hid_codes[:].bitcast(FP8X4),
+                        rhs_scale=hid_bytes[:],
+                        start=True,
+                        stop=True,
+                    )
+                result = work.tile([P, N // P, OUT_COLS], F32, name="result", align_bytes=64)
+                nc.scalar.copy(result[:].rearrange("p b j -> p (b j)"), total[:, 0 : (N // P) * OUT_COLS])
+                nc.sync.dma_start(out_rows[:, :, cols], result[:])

from contextlib import ExitStack

import concourse.mybir as mybir
from concourse.masks import make_identity

K, T, S, N, H = 512, 1024, 512, 256, 512
FLOPS = 2 * K * H * S * 2 + 2 * H * N * S

F32 = mybir.dt.float32
BF16 = mybir.dt.bfloat16
I32 = mybir.dt.int32
U32 = mybir.dt.uint32
U16 = mybir.dt.uint16
U8 = mybir.dt.uint8
FP8X4 = mybir.dt.float8_e4m3fn_x4
FP4X4 = mybir.dt.float4_e2m1fn_x4
ALU = mybir.AluOpType
ACT = mybir.ActivationFunctionType

P = 128
PACK = 4
GROUP = 16
X, Y = 0, 1
HALF = S // 2
OUT_COLS = 128
LINE = 4
Z_SCALE = 1.140625 / 40.0


def tile_picked_ypolym_vir_p_kernel(
    tc, x_words, x_scales, w1_words, w1_scales, w2_words, w2_scales, unit, w3_words, w3_scales, offs, nxt, prv, out
):
    nc = tc.nc
    planes = range(PACK)
    with ExitStack() as ctx:
        held = ctx.enter_context(tc.tile_pool(name="held", bufs=1))
        work = ctx.enter_context(tc.tile_pool(name="work", bufs=PACK))
        psum = ctx.enter_context(tc.psum_pool(name="psum", bufs=2))

        offs_sb = held.tile([P, S // GROUP], U16, name="offs_sb")
        nxt_sb = held.tile([P, S // GROUP], U16, name="nxt_sb")
        prv_sb = held.tile([P, S // GROUP], U16, name="prv_sb")
        x_codes = held.tile([P, T], U32, name="x_codes", align_bytes=64)
        x_bytes = held.tile([P, T], U8, name="x_bytes", align_bytes=64)
        w12_codes = held.tile([P, 2, 2 * H], U8, name="w12_codes", align_bytes=64)
        w3_codes = held.tile([P, 2 * N], U8, name="w3_codes", align_bytes=64)
        w_bytes = held.tile([P, 2 * H + N], U8, name="w_bytes", align_bytes=64)
        unit_sb = held.tile([P, PACK], F32, name="unit_sb")
        coords = held.tile([P, (2 * PACK + 1) * S], F32, name="coords", align_bytes=64)
        ident = held.tile([P, P], F32, name="ident", align_bytes=64)

        def first_column(t, w):
            return (2 * (PACK - 1 - t) + 1 - w) * S

        nc.vector.memset(x_bytes[:].bitcast(I32), 0)
        nc.vector.memset(w_bytes[:].bitcast(I32), 0)
        nc.vector.memset(coords[:, 2 * PACK * S :], 0.0)
        make_identity(nc, ident[:])

        def load_scale_rows(dst, src):
            for q in range(4):
                nc.sync.dma_start(dst[32 * q : 32 * q + 4, :].bitcast(I32), src[0, 4 * q : 4 * q + 4, :].bitcast(I32))

        nc.sync.dma_start(offs_sb[:], offs)
        nc.sync.dma_start(w12_codes[:, X, :].bitcast(I32), w1_words[0].bitcast(I32))
        nc.sync.dma_start(w12_codes[:, Y, :].bitcast(I32), w2_words[0].bitcast(I32))
        nc.sync.dma_start(x_codes[:].bitcast(I32), x_words[0].rearrange("p n t -> p (n t)").bitcast(I32))
        load_scale_rows(x_bytes, x_scales)
        load_scale_rows(w_bytes[:, 0:H], w1_scales)
        load_scale_rows(w_bytes[:, H : 2 * H], w2_scales)
        nc.sync.dma_start(nxt_sb[:], nxt)
        nc.sync.dma_start(prv_sb[:], prv)
        nc.sync.dma_start(unit_sb[:], unit.rearrange("(p t) o -> p (t o)", t=PACK))
        nc.sync.dma_start(w3_codes[:].bitcast(I32), w3_words[0].bitcast(I32))
        load_scale_rows(w_bytes[:, 2 * H :], w3_scales)

        dealt_codes = held.tile([P, 2, PACK, 2 * P], U8, name="dealt_codes", align_bytes=64)
        dealt_bytes = held.tile([P, 2, PACK, P], U8, name="dealt_bytes", align_bytes=64)
        for w in (X, Y):
            nc.vector.tensor_copy(
                dealt_codes[:, w, :, :].rearrange("p t (m b) -> p t m b", b=2),
                w12_codes[:, w, :].rearrange("p (m t b) -> p t m b", t=PACK, b=2),
            )

        picked_codes = held.tile([P, S], U32, name="picked_codes", align_bytes=64)
        picked_bytes = held.tile([P, S], U8, name="picked_bytes", align_bytes=64)
        nc.vector.tensor_copy(picked_codes[:], x_codes[:].indirect(offs_sb[:]))
        nc.vector.tensor_copy(picked_bytes[:], x_bytes[:].indirect(offs_sb[:]))

        by_plane = w_bytes[:, 0 : 2 * H].rearrange("p (w m t) -> p w t m", w=2, t=PACK)
        nc.vector.tensor_copy(dealt_bytes[:, :, 0:1, :], by_plane[:, :, 0:1, :])
        nc.vector.tensor_copy(dealt_bytes[:, :, 1:PACK, :], by_plane[:, :, 1:PACK, :])

        vir_unit = held.tile([P, PACK], F32, name="vir_unit")
        bend_unit = held.tile([P, PACK], F32, name="bend_unit")
        nc.gpsimd.tensor_scalar(vir_unit[:], unit_sb[:], -360.0 * Z_SCALE, 0.0, ALU.mult, ALU.add)
        nc.gpsimd.tensor_scalar(bend_unit[:], unit_sb[:], -0.3, 0.0, ALU.mult, ALU.add)

        shift = held.tile([P, 1], F32, name="shift")
        nc.gpsimd.memset(shift[:], 1.0)
        warm = held.tile([P, 1], F32, name="warm")
        nc.scalar.activation(warm[:], shift[:], ACT.Abs_reciprocal_sqrt)
        nc.gpsimd.tensor_scalar(shift[:], shift[:], -1.0 / (36.0 * Z_SCALE), 0.0, ALU.mult, ALU.add)

        def turn(dst, terms):
            for c in range(S // P):
                cols = slice(c * P, (c + 1) * P)
                for n, term in enumerate(terms):
                    nc.tensor.matmul(
                        dst[:, cols],
                        lhsT=term(cols),
                        rhs=ident[:],
                        start=(n == 0),
                        stop=(n == len(terms) - 1),
                        is_transpose=True,
                    )

        bonds = []
        for t in planes:
            sums = [psum.tile([P, S], F32, name="sums", tag=("px", "py")[w]) for w in (X, Y)]
            for w in (X, Y):
                nc.tensor.matmul_mx(
                    out=sums[w][:],
                    lhsT=dealt_codes[:, w, t, :].bitcast(FP4X4),
                    lhsT_scale=dealt_bytes[:, w, t, :],
                    rhs=picked_codes[:].bitcast(FP8X4),
                    rhs_scale=picked_bytes[:],
                    start=True,
                    stop=True,
                )
                own = coords[:, first_column(t, w) : first_column(t, w) + S]
                if w == X:
                    nc.scalar.copy(own, sums[w][:])
                else:
                    nc.vector.tensor_copy(own, sums[w][:])
            ahead = work.tile([P, 2, S], F32, name="ahead", align_bytes=64)
            behind = work.tile([P, 2, S], F32, name="behind", align_bytes=64)
            bond = work.tile([P, 4, S], F32, name="bond", align_bytes=64)
            windows = [coords[:, first_column(t, w) : first_column(t, w) + 2 * S] for w in (X, Y)]
            for w in (X, Y):
                nc.vector.tensor_copy(ahead[:, w, :], windows[w].indirect(nxt_sb[:]))
            for w in (X, Y):
                nc.vector.tensor_tensor(bond[:, 1 - w, :], ahead[:, w, :], sums[w][:], ALU.subtract)
            for w in (X, Y):
                nc.scalar.activation(behind[:, 1 - w, :], windows[w].indirect(prv_sb[:]), ACT.Copy)
            if t == 0:
                for w in (X, Y):
                    nc.gpsimd.tensor_tensor(bond[:, 3 - w, :], behind[:, 1 - w, :], windows[w][:, 0:S], ALU.subtract)
            else:
                both = windows[Y].rearrange("p (w s) -> p w s", w=2)
                nc.gpsimd.tensor_tensor(bond[:, 2:4, :], behind[:], both, ALU.subtract)
            bonds.append(bond)

        squares, inverses = [], []
        for t in planes:
            square = work.tile([P, 2, S], F32, name="square", align_bytes=64)
            nc.scalar.activation(square[:], bonds[t][:, 0:2, :], ACT.Square)
            r2 = psum.tile([P, S], F32, name="r2", tag="turned")
            turn(r2, [lambda cols: square[:, 0, cols], lambda cols: square[:, 1, cols]])
            z2 = work.tile([P, S], F32, name="z2", align_bytes=64)
            inverse = work.tile([P, S], F32, name="inverse", align_bytes=64)
            nc.scalar.activation(z2[:], r2[:], ACT.Square, bias=40.0 * Z_SCALE, scale=Z_SCALE)
            nc.scalar.activation(inverse[:], z2[:], ACT.Abs_reciprocal_sqrt)
            squares.append(square)
            inverses.append(inverse)

        stiffs, dots = [], []
        for t in planes:
            stiff = psum.tile([P, S], F32, name="stiff", tag=("stiff", "stiff", "px", "py")[t])
            turn(stiff, [lambda cols: shift[:].to_broadcast([P, P]), lambda cols: inverses[t][:, cols]])
            bond, factor = bonds[t], bend_unit[:, t : t + 1]
            terms = work.tile([P, 2, S], F32, name="terms", align_bytes=64)
            dot = work.tile([P, S], F32, name="dot", align_bytes=64)
            if t == 0:
                plain_dot = held.tile([P, S], F32, name="plain_dot", align_bytes=64)
                nc.gpsimd.tensor_tensor(terms[:], bond[:, 0:2, :], bond[:, 2:4, :], ALU.mult)
                nc.gpsimd.tensor_tensor(plain_dot[:], terms[:, 0, :], terms[:, 1, :], ALU.add)
                nc.gpsimd.tensor_scalar(dot[:], plain_dot[:], factor, 0.0, ALU.mult, ALU.add)
            else:
                for n in range(2):
                    nc.vector.scalar_tensor_tensor(
                        terms[:, n, :], bond[:, n, :], factor, bond[:, 2 + n, :], ALU.mult, ALU.mult
                    )
                nc.vector.tensor_tensor(dot[:], terms[:, 0, :], terms[:, 1, :], ALU.add)
            stiffs.append(stiff)
            dots.append(dot)

        vir = held.tile([P, PACK, S], F32, name="vir", align_bytes=64)
        bend = held.tile([P, PACK, S], F32, name="bend", align_bytes=64)
        out_rows = out.rearrange("(b p) j -> p b j", p=P)
        for first in range(0, S, HALF):
            half = slice(first, first + HALF)
            entries = nxt_sb[:, first // GROUP : (first + HALF) // GROUP]
            for t in planes:
                nc.scalar.activation(bend[:, t, half], dots[t][:].indirect(entries), ACT.Copy)
                nc.vector.scalar_tensor_tensor(
                    vir[:, t, half], stiffs[t][:, half], vir_unit[:, t : t + 1], squares[t][:, 1, half],
                    ALU.mult, ALU.mult,
                )
            for c0 in range(first, first + HALF, OUT_COLS):
                cols = slice(c0, c0 + OUT_COLS)
                hid = work.tile([P, OUT_COLS, PACK], BF16, name="hid", align_bytes=64)
                nc.vector.tensor_tensor(
                    hid[:].rearrange("p (c i) t -> p c t i", i=LINE),
                    vir[:, :, cols].rearrange("p t (c i) -> p c t i", i=LINE),
                    bend[:, :, cols].rearrange("p t (c i) -> p c t i", i=LINE),
                    ALU.add,
                )
                hid_codes = work.tile([P, OUT_COLS], U32, name="hid_codes", align_bytes=64)
                hid_bytes = work.tile([P, OUT_COLS], U8, name="hid_bytes", align_bytes=64)
                nc.vector.quantize_mx(
                    out=hid_codes[:].bitcast(FP8X4), scales=hid_bytes[:], in_=hid[:].rearrange("p c t -> p (c t)")
                )
                total = psum.tile([P, S], F32, name="total", tag="turned")
                for b in range(N // P):
                    nc.tensor.matmul_mx(
                        out=total[:, b * OUT_COLS : (b + 1) * OUT_COLS],
                        lhsT=w3_codes[:, 2 * b * P : 2 * (b + 1) * P].bitcast(FP4X4),
                        lhsT_scale=w_bytes[:, 2 * H + b * P : 2 * H + (b + 1) * P],
                        rhs=hid_codes[:].bitcast(FP8X4),
                        rhs_scale=hid_bytes[:],
                        start=True,
                        stop=True,
                    )
                result = work.tile([P, N // P, OUT_COLS], F32, name="result", align_bytes=64)
                nc.scalar.copy(result[:].rearrange("p b j -> p (b j)"), total[:, 0 : (N // P) * OUT_COLS])
                nc.sync.dma_start(out_rows[:, :, cols], result[:])
